import numpy as np
import ml_dtypes


def mxq(x, axis, fmt="e4m3"):
    dtype, down = {"e4m3": (ml_dtypes.float8_e4m3fn, 7), "e5m2": (ml_dtypes.float8_e5m2, 14)}[fmt]
    v = np.moveaxis(np.asarray(x, np.float32).astype(ml_dtypes.bfloat16).astype(np.float64), axis, -1)
    blocks = v.reshape(v.shape[:-1] + (-1, 32))
    amax = np.abs(blocks).max(-1, keepdims=True)
    byte = np.maximum(np.where(amax > 0, np.frexp(amax)[1] - 1 + 127, 0) - down, 1)
    scale = np.exp2(byte - 127.0)
    codes = (blocks / scale).astype(np.float32).astype(dtype).astype(np.float64)
    return np.moveaxis((codes * scale).reshape(v.shape), -1, axis)


WIDE = False


def mx_kscale(k):
    if not WIDE:
        return np.ones(k)
    levels = np.array([10, -10, 5, -5, 0])
    if k % 512:
        return np.exp2(np.random.permutation(np.resize(levels, k // 32))).repeat(32)
    a = np.empty((k // 512, 16))
    for p in range(k // 512):
        a[p, :8] = np.random.permutation(np.resize(levels, 8))
        for g in range(8):
            far = levels[np.abs(levels - a[p, g]) >= 10]
            a[p, g + 8] = far[np.random.randint(len(far))]
    return np.exp2(a.ravel()).repeat(32)


def f64(x):
    return np.asarray(x).astype(np.float64)


def striped(idx):
    return np.tile(idx.reshape(-1, 16).T, (8, 1)).astype(np.uint16)


def unstriped(offs):
    return offs[:16].T.reshape(-1).astype(np.int64)


def striped8(idx):
    return np.concatenate([x.reshape(-1, 16).T for x in idx]).astype(np.uint16)


def runs(offs, k):
    lists = np.stack([offs[16 * r : 16 * r + 16].T.reshape(-1) for r in range(8)]).astype(np.int64)
    return lists[np.arange(k) % 512 // 64]


def pack_weight(w):
    k, n = w.shape
    w = f64(np.asarray(w, np.float32).astype(ml_dtypes.bfloat16)).reshape(k // 32, 32, n)
    amax = np.abs(w).max(1)
    byte = np.clip(np.where(amax > 0, np.frexp(amax)[1] - 1 + 127 - 7, 1), 1, 254)
    scaled = (w * np.exp2(127.0 - byte)[:, None, :]).reshape(k, n).astype(np.float32)
    words = np.ascontiguousarray(scaled.reshape(k // 512, 128, 4, n).transpose(0, 1, 3, 2)).astype(ml_dtypes.float8_e4m3fn).view(np.uint8)
    return words, np.ascontiguousarray(byte.astype(np.uint8).reshape(k // 512, 16, n))


def unpack_weight(words, scales):
    g, p, n, _ = words.shape
    vals = np.ascontiguousarray(words).view(ml_dtypes.float8_e4m3fn).astype(np.float64) * np.repeat(np.exp2(scales.astype(np.float64) - 127.0), 8, axis=1)[..., None]
    return vals.transpose(0, 1, 3, 2).reshape(g * 512, n)


K, T, S, G, H, W = 512, 2048, 512, 2048, 512, 256


def setup_inputs():
    n = np.random.standard_normal
    s = mx_kscale(K)[:, None]
    packed_xT = pack_weight(n((K, T)) * s)
    packed_dT = pack_weight(n((K, G)) / s)
    perm = np.stack([np.random.permutation(S) for _ in range(8)])
    return {
        "x_words": packed_xT[0],
        "x_scales": packed_xT[1],
        "d_words": packed_dT[0],
        "d_scales": packed_dT[1],
        "gs": (np.random.uniform(0.5, 1.5, (K, 1)) * s).astype(np.float32),
        "offs": striped(np.random.permutation(T)[:S]),
        "ci": striped(np.random.permutation(G)[:H]),
        "k1": striped8(np.random.randint(0, G, (8, H))),
        "n1": striped8(perm[:, :W]),
        "n2": striped8(perm[:, W:]),
        "n3": striped8(np.stack([np.random.permutation(S) for _ in range(8)])),
    }


def reference(x_words, x_scales, d_words, d_scales, gs, offs, ci, k1, n1, n2, n3):
    d_k1 = unpack_weight(d_words, d_scales)[np.arange(K)[:, None], runs(k1, K)]
    d_ci = unpack_weight(d_words, d_scales)[:, unstriped(ci)]
    xq = unpack_weight(x_words, x_scales)[:, unstriped(offs)]
    s = 0.0625 * (d_ci.T @ xq)
    z = f64(gs) * s
    h = 0.0625 * ((d_k1.T @ mxq(z, 0, "e4m3")))
    pa = h[np.arange(H)[:, None], runs(n1, H)]
    pb = h[np.arange(H)[:, None], runs(n2, H)]
    rb = np.minimum(pa, pb)
    ra = np.maximum(pa, pb)
    ds = np.zeros((H, S))
    ds[np.arange(H)[:, None], runs(n1, H)] = ra
    dt = ds.copy()
    dt[np.arange(H)[:, None], runs(n2, H)] = rb
    return dt - (dt[np.arange(H)[:, None], runs(n3, H)])

@@ -1,0 +1,205 @@
+from contextlib import ExitStack
+
+import concourse.mybir as mybir
+
+F32 = mybir.dt.float32
+BF16 = mybir.dt.bfloat16
+I32 = mybir.dt.int32
+U32 = mybir.dt.uint32
+U16 = mybir.dt.uint16
+U8 = mybir.dt.uint8
+FP8X4 = mybir.dt.float8_e4m3fn_x4
+ALU = mybir.AluOpType
+COPY = mybir.ActivationFunctionType.Copy
+
+P = 128
+PACK = 4
+TABLE = 2048
+S = 512
+HALF = 256
+QUARTER = 128
+SIXTEENTH = 0.0625
+FLOPS = 2 * 2 * 512 * 512 * 512
+
+
+def tile_picked_dwqiordd_none_p_kernel(
+    tc, x_words, x_scales, d_words, d_scales, gs, offs, ci, k1, n1, n2, n3, out
+):
+    nc = tc.nc
+    with ExitStack() as ctx:
+        keep = ctx.enter_context(tc.tile_pool(name="keep", bufs=1))
+        psum = ctx.enter_context(tc.psum_pool(name="psum", bufs=1))
+
+        def load_list(src, name):
+            tile = keep.tile([P, src.shape[1]], U16, name=name)
+            nc.sync.dma_start(tile[:], src)
+            return tile
+
+        def words_of(src):
+            return src[0].rearrange("p n t -> p (n t)").bitcast(I32)
+
+        def dealt(ap):
+            return ap.rearrange("p (t m) -> p m t", t=PACK)
+
+        def in_order(ap):
+            return ap.rearrange("p (m t) -> p m t", t=PACK)
+
+        d_sc = keep.tile([P, TABLE], U8, name="d_sc")
+        x_sc = keep.tile([P, TABLE], U8, name="x_sc")
+        d_w = keep.tile([P, TABLE], U32, name="d_w")
+        x_w = keep.tile([P, TABLE], U32, name="x_w", tag="x_w")
+        nc.vector.memset(d_sc[:].bitcast(I32), 0)
+        nc.vector.memset(x_sc[:].bitcast(I32), 0)
+
+        ci_l = load_list(ci, "ci_l")
+        k1_l = load_list(k1, "k1_l")
+        d_rows2 = d_scales[0].bitcast(I32).rearrange("(m j) c -> j m c", j=2)
+        d_rows4 = d_scales[0].bitcast(I32).rearrange("(q j) c -> j q c", j=4)
+        x_rows4 = x_scales[0].bitcast(I32).rearrange("(q j) c -> j q c", j=4)
+        for j in range(2):
+            nc.sync.dma_start(d_sc[:].bitcast(I32)[j:P:16, :], d_rows2[j])
+        for j in range(2, 4):
+            nc.sync.dma_start(d_sc[:].bitcast(I32)[j:P:32, :], d_rows4[j])
+        nc.sync.dma_start(d_w[:].bitcast(I32), words_of(d_words))
+        offs_l = load_list(offs, "offs_l")
+        for j in range(4):
+            nc.sync.dma_start(x_sc[:].bitcast(I32)[j:P:32, :], x_rows4[j])
+        nc.sync.dma_start(x_w[:].bitcast(I32), words_of(x_words))
+        gs_t = keep.tile([P, PACK], F32, name="gs_t")
+        nc.sync.dma_start(gs_t[:], gs.rearrange("(p t) o -> p (t o)", t=PACK))
+        n1_l = load_list(n1, "n1_l")
+        n2_l = load_list(n2, "n2_l")
+        n3_l = load_list(n3, "n3_l")
+
+        gain = keep.tile([P, PACK], F32, name="gain")
+        nc.scalar.activation(gain[:], gs_t[:], COPY, scale=SIXTEENTH)
+
+        ci_s = keep.tile([P, S], U8, name="ci_s", align_bytes=64)
+        ci_w = keep.tile([P, S], U32, name="ci_w", align_bytes=64)
+        k1_sg = keep.tile([P, S], U8, name="k1_sg")
+        k1_s = keep.tile([P, S], U8, name="k1_s", align_bytes=64)
+        k1_w = keep.tile([P, S], U32, name="k1_w", align_bytes=64)
+        xq_s = keep.tile([P, S], U8, name="xq_s", align_bytes=64)
+        xq_w = [keep.tile([P, HALF], U32, name="xq_w%d" % h, align_bytes=64) for h in range(2)]
+
+        nc.vector.tensor_copy(dealt(ci_s[:]), d_sc[:].indirect(ci_l[:]))
+        nc.vector.tensor_copy(k1_sg[:], d_sc[:].indirect(k1_l[:]))
+        nc.vector.tensor_copy(dealt(k1_s[:]), in_order(k1_sg[:]))
+        nc.vector.tensor_copy(dealt(ci_w[:]), d_w[:].indirect(ci_l[:]))
+        for j in range(2):
+            nc.sync.dma_start(k1_s[:].bitcast(I32)[2 + j : P : 32, :], k1_s[:].bitcast(I32)[16 + j : P : 32, :])
+        nc.vector.tensor_copy(xq_s[:], x_sc[:].indirect(offs_l[:]))
+        for h in range(2):
+            cols = offs_l[:, h * 16 : (h + 1) * 16]
+            nc.vector.tensor_copy(xq_w[h][:], x_w[:].indirect(cols))
+
+        def score(dst, t, h, lo, n):
+            nc.tensor.matmul_mx(
+                out=dst,
+                lhsT=ci_w[:, t * P : (t + 1) * P].bitcast(FP8X4),
+                lhsT_scale=ci_s[:, t * P : (t + 1) * P],
+                rhs=xq_w[h][:, lo : lo + n].bitcast(FP8X4),
+                rhs_scale=xq_s[:, h * HALF + lo : h * HALF + lo + n],
+                start=True,
+                stop=True,
+            )
+
+        z_in = [keep.tile([P, HALF, PACK], BF16, name="z_in%d" % h, align_bytes=64) for h in range(2)]
+        z_rows = keep.tile([P, PACK, HALF], BF16, name="z_rows")
+        for u in range(2):
+            bank = psum.tile([P, 2, HALF], F32, name="s_a%d" % u)
+            for v in range(2):
+                score(bank[:, v, :], 2 * u + v, 0, 0, HALF)
+            for v in range(2):
+                t = 2 * u + v
+                nc.scalar.activation(z_rows[:, t, :], bank[:, v, :], COPY, scale=gain[:, t : t + 1])
+        nc.scalar.copy(z_in[0][:], z_rows[:].rearrange("p t j -> p j t"))
+
+        k1_wg = keep.tile([P, S], U32, name="k1_wg", tag="x_w")
+        nc.vector.tensor_copy(k1_wg[:], d_w[:].indirect(k1_l[:]))
+        nc.vector.tensor_copy(dealt(k1_w[:]), in_order(k1_wg[:]))
+
+        for u in range(2):
+            bank = psum.tile([P, PACK, QUARTER], F32, name="s_b%d" % u)
+            for t in range(PACK):
+                score(bank[:, t, :], t, 1, u * QUARTER, QUARTER)
+            nc.vector.tensor_tensor(
+                z_in[1][:, u * QUARTER : (u + 1) * QUARTER, :],
+                bank[:].rearrange("p t j -> p j t"),
+                gain[:].unsqueeze(1).to_broadcast([P, QUARTER, PACK]),
+                ALU.mult,
+            )
+
+        z_w = keep.tile([P, S], U32, name="z_w", align_bytes=64)
+        z_s = keep.tile([P, S], U8, name="z_s", align_bytes=64)
+        for h in (1, 0):
+            nc.vector.quantize_mx(
+                out=z_w[:, h * HALF : (h + 1) * HALF].bitcast(FP8X4),
+                scales=z_s[:, h * HALF : (h + 1) * HALF],
+                in_=z_in[h][:].rearrange("p j t -> p (j t)"),
+            )
+
+        def layer(dst, t, lo, n):
+            nc.tensor.matmul_mx(
+                out=dst,
+                lhsT=k1_w[:, t * P : (t + 1) * P].bitcast(FP8X4),
+                lhsT_scale=k1_s[:, t * P : (t + 1) * P],
+                rhs=z_w[:, lo : lo + n].bitcast(FP8X4),
+                rhs_scale=z_s[:, lo : lo + n],
+                start=True,
+                stop=True,
+            )
+
+        out_rows = out.rearrange("(p t) j -> p t j", t=PACK)
+        hid = [keep.tile([P, S], F32, name="hid%d" % t) for t in range(PACK)]
+        pa = [keep.tile([P, HALF], F32, name="pa%d" % t) for t in range(PACK)]
+        pb = [keep.tile([P, HALF], F32, name="pb%d" % t) for t in range(PACK)]
+        hi = [keep.tile([P, HALF], F32, name="hi%d" % t) for t in range(PACK)]
+        lo = [keep.tile([P, HALF], F32, name="lo%d" % t) for t in range(PACK)]
+        srt = [keep.tile([P, S], F32, name="srt%d" % t) for t in range(PACK)]
+        far = [keep.tile([P, S], F32, name="far%d" % t) for t in range(PACK)]
+        res = [keep.tile([P, S], F32, name="res%d" % t) for t in range(PACK)]
+
+        def produce(t):
+            if t == 0:
+                for h in (1, 0):
+                    bank = psum.tile([P, S], F32, name="h_bank", tag="h%d" % (1 - h))
+                    layer(bank[:, :HALF], t, h * HALF, HALF)
+                    nc.scalar.activation(hid[t][:, h * HALF : (h + 1) * HALF], bank[:, :HALF], COPY, scale=SIXTEENTH)
+                nc.vector.tensor_copy(pa[t][:], hid[t][:].indirect(n1_l[:]))
+            else:
+                bank = psum.tile([P, S], F32, name="h_bank", tag="h1")
+                layer(bank[:], t, 0, S)
+                nc.scalar.activation(hid[t][:], bank[:], COPY, scale=SIXTEENTH)
+                nc.scalar.activation(pa[t][:], hid[t][:].indirect(n1_l[:]), COPY)
+            nc.scalar.activation(pb[t][:], hid[t][:].indirect(n2_l[:]), COPY)
+
+        def finish(t):
+            for h in range(2):
+                cols = slice(h * HALF, (h + 1) * HALF)
+                nc.scalar.activation(far[t][:, cols], srt[t][:].indirect(n3_l[:, h * 16 : (h + 1) * 16]), COPY)
+            if t < PACK - 1:
+                nc.vector.tensor_tensor(res[t][:], srt[t][:], far[t][:], ALU.subtract)
+                nc.sync.dma_start(out_rows[:, t, :], res[t][:])
+            else:
+                for h in range(2):
+                    cols = slice(h * HALF, (h + 1) * HALF)
+                    nc.vector.tensor_tensor(res[t][:, cols], srt[t][:, cols], far[t][:, cols], ALU.subtract)
+                    nc.sync.dma_start(out_rows[:, t, cols], res[t][:, cols])
+
+        produce(0)
+        produce(1)
+        nc.vector.tensor_tensor(hi[0][:], pa[0][:], pb[0][:], ALU.max)
+        nc.vector.tensor_tensor(lo[0][:], pa[0][:], pb[0][:], ALU.min)
+        for t in range(PACK):
+            if t + 2 < PACK:
+                produce(t + 2)
+            nc.vector.tensor_copy(srt[t][:].indirect(n1_l[:]), hi[t][:])
+            if t + 1 < PACK:
+                nc.vector.tensor_tensor(hi[t + 1][:], pa[t + 1][:], pb[t + 1][:], ALU.max)
+            if t > 0:
+                finish(t - 1)
+            nc.vector.tensor_copy(srt[t][:].indirect(n2_l[:]), lo[t][:])
+            if t + 1 < PACK:
+                nc.vector.tensor_tensor(lo[t + 1][:], pa[t + 1][:], pb[t + 1][:], ALU.min)
+        finish(PACK - 1)

@@ -78,7 +78,7 @@ def tile_picked_dwqiordd_none_p_kernel(
         ci_w = keep.tile([P, S], U32, name="ci_w", align_bytes=64)
         k1_sg = keep.tile([P, S], U8, name="k1_sg")
         k1_s = keep.tile([P, S], U8, name="k1_s", align_bytes=64)
-        k1_w = keep.tile([P, S], U32, name="k1_w", align_bytes=64)
+        k1_w0 = keep.tile([P, P], U32, name="k1_w0", align_bytes=64)
         xq_s = keep.tile([P, S], U8, name="xq_s", align_bytes=64)
         xq_w = [keep.tile([P, HALF], U32, name="xq_w%d" % h, align_bytes=64) for h in range(2)]
 
@@ -104,8 +104,8 @@ def tile_picked_dwqiordd_none_p_kernel(
                 stop=True,
             )
 
-        z_in = [keep.tile([P, HALF, PACK], BF16, name="z_in%d" % h, align_bytes=64) for h in range(2)]
-        z_rows = keep.tile([P, PACK, HALF], BF16, name="z_rows")
+        z_in = [keep.tile([P, HALF, PACK], BF16, name="z_in%d" % h, tag="hid%d" % (5 * h), align_bytes=64) for h in range(2)]
+        z_rows = keep.tile([P, PACK, HALF], BF16, name="z_rows", tag="z_rows", align_bytes=64)
         for u in range(2):
             bank = psum.tile([P, 2, HALF], F32, name="s_a%d" % u)
             for v in range(2):
@@ -117,7 +117,7 @@ def tile_picked_dwqiordd_none_p_kernel(
 
         k1_wg = keep.tile([P, S], U32, name="k1_wg", tag="x_w")
         nc.vector.tensor_copy(k1_wg[:], d_w[:].indirect(k1_l[:]))
-        nc.vector.tensor_copy(dealt(k1_w[:]), in_order(k1_wg[:]))
+        nc.vector.tensor_copy(k1_w0[:], in_order(k1_wg[:])[:, :, 0])
 
         for u in range(2):
             bank = psum.tile([P, PACK, QUARTER], F32, name="s_b%d" % u)
@@ -132,17 +132,20 @@ def tile_picked_dwqiordd_none_p_kernel(
 
         z_w = keep.tile([P, S], U32, name="z_w", align_bytes=64)
         z_s = keep.tile([P, S], U8, name="z_s", align_bytes=64)
-        for h in (1, 0):
+        for h, a, b in ((1, 0, QUARTER), (1, QUARTER, HALF), (0, 0, HALF)):
             nc.vector.quantize_mx(
-                out=z_w[:, h * HALF : (h + 1) * HALF].bitcast(FP8X4),
-                scales=z_s[:, h * HALF : (h + 1) * HALF],
-                in_=z_in[h][:].rearrange("p j t -> p (j t)"),
+                out=z_w[:, h * HALF + a : h * HALF + b].bitcast(FP8X4),
+                scales=z_s[:, h * HALF + a : h * HALF + b],
+                in_=z_in[h][:, a:b, :].rearrange("p j t -> p (j t)"),
             )
+        k1_wr = keep.tile([P, PACK - 1, P], U32, name="k1_wr", tag="z_rows", align_bytes=64)
+        nc.vector.tensor_copy(k1_wr[:].rearrange("p t m -> p m t"), in_order(k1_wg[:])[:, :, 1:])
+        k1_w = [k1_w0[:]] + [k1_wr[:, t, :] for t in range(PACK - 1)]
 
         def layer(dst, t, lo, n):
             nc.tensor.matmul_mx(
                 out=dst,
-                lhsT=k1_w[:, t * P : (t + 1) * P].bitcast(FP8X4),
+                lhsT=k1_w[t].bitcast(FP8X4),
                 lhsT_scale=k1_s[:, t * P : (t + 1) * P],
                 rhs=z_w[:, lo : lo + n].bitcast(FP8X4),
                 rhs_scale=z_s[:, lo : lo + n],
@@ -151,55 +154,70 @@ def tile_picked_dwqiordd_none_p_kernel(
             )
 
         out_rows = out.rearrange("(p t) j -> p t j", t=PACK)
-        hid = [keep.tile([P, S], F32, name="hid%d" % t) for t in range(PACK)]
-        pa = [keep.tile([P, HALF], F32, name="pa%d" % t) for t in range(PACK)]
+        hid = [keep.tile([P, S], F32, name="hid%d" % t, tag="hid%d" % t, align_bytes=64) for t in range(PACK)]
+        pa = [keep.tile([P, HALF], F32, name="pa%d" % t, tag="pa%d" % t, align_bytes=64) for t in range(PACK)]
         pb = [keep.tile([P, HALF], F32, name="pb%d" % t) for t in range(PACK)]
         hi = [keep.tile([P, HALF], F32, name="hi%d" % t) for t in range(PACK)]
-        lo = [keep.tile([P, HALF], F32, name="lo%d" % t) for t in range(PACK)]
         srt = [keep.tile([P, S], F32, name="srt%d" % t) for t in range(PACK)]
         far = [keep.tile([P, S], F32, name="far%d" % t) for t in range(PACK)]
-        res = [keep.tile([P, S], F32, name="res%d" % t) for t in range(PACK)]
+
+        def pairs(lst, a, b):
+            return lst[:, a // 16 : b // 16]
+
+        def fetch(t, a, b, first):
+            if first:
+                nc.vector.tensor_copy(pa[t][:, a:b], hid[t][:].indirect(pairs(n1_l, a, b)))
+            else:
+                nc.scalar.activation(pa[t][:, a:b], hid[t][:].indirect(pairs(n1_l, a, b)), COPY)
+            nc.scalar.activation(pb[t][:, a:b], hid[t][:].indirect(pairs(n2_l, a, b)), COPY)
 
         def produce(t):
             if t == 0:
                 for h in (1, 0):
                     bank = psum.tile([P, S], F32, name="h_bank", tag="h%d" % (1 - h))
                     layer(bank[:, :HALF], t, h * HALF, HALF)
-                    nc.scalar.activation(hid[t][:, h * HALF : (h + 1) * HALF], bank[:, :HALF], COPY, scale=SIXTEENTH)
-                nc.vector.tensor_copy(pa[t][:], hid[t][:].indirect(n1_l[:]))
+                    cols = slice(h * HALF, (h + 1) * HALF)
+                    if h == 1:
+                        nc.vector.tensor_scalar(hid[t][:, cols], bank[:, :HALF], SIXTEENTH, None, ALU.mult)
+                    else:
+                        nc.scalar.activation(hid[t][:, cols], bank[:, :HALF], COPY, scale=SIXTEENTH)
+                fetch(t, 0, QUARTER, True)
+                fetch(t, QUARTER, HALF, False)
             else:
                 bank = psum.tile([P, S], F32, name="h_bank", tag="h1")
                 layer(bank[:], t, 0, S)
                 nc.scalar.activation(hid[t][:], bank[:], COPY, scale=SIXTEENTH)
-                nc.scalar.activation(pa[t][:], hid[t][:].indirect(n1_l[:]), COPY)
-            nc.scalar.activation(pb[t][:], hid[t][:].indirect(n2_l[:]), COPY)
+                fetch(t, 0, HALF, False)
 
-        def finish(t):
-            for h in range(2):
-                cols = slice(h * HALF, (h + 1) * HALF)
-                nc.scalar.activation(far[t][:, cols], srt[t][:].indirect(n3_l[:, h * 16 : (h + 1) * 16]), COPY)
-            if t < PACK - 1:
-                nc.vector.tensor_tensor(res[t][:], srt[t][:], far[t][:], ALU.subtract)
-                nc.sync.dma_start(out_rows[:, t, :], res[t][:])
-            else:
-                for h in range(2):
-                    cols = slice(h * HALF, (h + 1) * HALF)
-                    nc.vector.tensor_tensor(res[t][:, cols], srt[t][:, cols], far[t][:, cols], ALU.subtract)
-                    nc.sync.dma_start(out_rows[:, t, cols], res[t][:, cols])
+        def larger(t, a, b):
+            nc.vector.tensor_tensor(hi[t][:, a:b], pa[t][:, a:b], pb[t][:, a:b], ALU.max)
 
-        produce(0)
-        produce(1)
-        nc.vector.tensor_tensor(hi[0][:], pa[0][:], pb[0][:], ALU.max)
-        nc.vector.tensor_tensor(lo[0][:], pa[0][:], pb[0][:], ALU.min)
+        def look(t):
+            for a in (0, HALF):
+                nc.scalar.activation(far[t][:, a : a + HALF], srt[t][:].indirect(pairs(n3_l, a, a + HALF)), COPY)
+
+        def finish(engine, queue, t, tag, pieces):
+            res = keep.tile([P, S], F32, name="res%d" % t, tag=tag, align_bytes=64)
+            width = S // pieces
+            for a in range(0, S, width):
+                cols = slice(a, a + width)
+                engine.tensor_tensor(res[:, cols], srt[t][:, cols], far[t][:, cols], ALU.subtract)
+                queue.dma_start(out_rows[:, t, cols], res[:, cols])
+
+        steps = [(0, 0, QUARTER), (0, QUARTER, HALF)] + [(t, 0, HALF) for t in range(1, PACK)]
         for t in range(PACK):
-            if t + 2 < PACK:
-                produce(t + 2)
-            nc.vector.tensor_copy(srt[t][:].indirect(n1_l[:]), hi[t][:])
-            if t + 1 < PACK:
-                nc.vector.tensor_tensor(hi[t + 1][:], pa[t + 1][:], pb[t + 1][:], ALU.max)
-            if t > 0:
-                finish(t - 1)
-            nc.vector.tensor_copy(srt[t][:].indirect(n2_l[:]), lo[t][:])
-            if t + 1 < PACK:
-                nc.vector.tensor_tensor(lo[t + 1][:], pa[t + 1][:], pb[t + 1][:], ALU.min)
-        finish(PACK - 1)
+            produce(t)
+        larger(*steps[0])
+        for n, (t, a, b) in enumerate(steps):
+            nc.vector.tensor_copy(srt[t][:].indirect(pairs(n1_l, a, b)), hi[t][:, a:b])
+            lo = keep.tile([P, b - a], F32, name="lo%d" % n, tag="hid%d" % n, align_bytes=64)
+            nc.vector.tensor_tensor(lo[:], pa[t][:, a:b], pb[t][:, a:b], ALU.min)
+            for nxt in steps[n + 1 : n + 2]:
+                larger(*nxt)
+            nc.vector.tensor_copy(srt[t][:].indirect(pairs(n2_l, a, b)), lo[:])
+            if b == HALF:
+                look(t)
+            if t in (1, 2):
+                finish(nc.gpsimd, nc.gpsimd, t - 1, "pa%d" % t, 1)
+        finish(nc.vector, nc.sync, 2, "hid4", 1)
+        finish(nc.vector, nc.sync, 3, "res3", 2)

@@ -59,7 +59,7 @@ def tile_picked_dwqiordd_none_p_kernel(
         for j in range(2):
             nc.sync.dma_start(d_sc[:].bitcast(I32)[j:P:16, :], d_rows2[j])
         for j in range(2, 4):
-            nc.sync.dma_start(d_sc[:].bitcast(I32)[j:P:32, :], d_rows4[j])
+            nc.scalar.dma_start(d_sc[:].bitcast(I32)[j:P:32, :], d_rows4[j])
         nc.sync.dma_start(d_w[:].bitcast(I32), words_of(d_words))
         offs_l = load_list(offs, "offs_l")
         for j in range(4):
@@ -77,17 +77,17 @@ def tile_picked_dwqiordd_none_p_kernel(
         ci_s = keep.tile([P, S], U8, name="ci_s", align_bytes=64)
         ci_w = keep.tile([P, S], U32, name="ci_w", align_bytes=64)
         k1_sg = keep.tile([P, S], U8, name="k1_sg")
-        k1_s = keep.tile([P, S], U8, name="k1_s", align_bytes=64)
         k1_w0 = keep.tile([P, P], U32, name="k1_w0", align_bytes=64)
         xq_s = keep.tile([P, S], U8, name="xq_s", align_bytes=64)
         xq_w = [keep.tile([P, HALF], U32, name="xq_w%d" % h, align_bytes=64) for h in range(2)]
 
-        nc.vector.tensor_copy(dealt(ci_s[:]), d_sc[:].indirect(ci_l[:]))
         nc.vector.tensor_copy(k1_sg[:], d_sc[:].indirect(k1_l[:]))
+        nc.vector.tensor_copy(dealt(ci_s[:]), d_sc[:].indirect(ci_l[:]))
+        k1_s = keep.tile([P, S], U8, name="k1_s", align_bytes=64)
         nc.vector.tensor_copy(dealt(k1_s[:]), in_order(k1_sg[:]))
-        nc.vector.tensor_copy(dealt(ci_w[:]), d_w[:].indirect(ci_l[:]))
         for j in range(2):
             nc.sync.dma_start(k1_s[:].bitcast(I32)[2 + j : P : 32, :], k1_s[:].bitcast(I32)[16 + j : P : 32, :])
+        nc.vector.tensor_copy(dealt(ci_w[:]), d_w[:].indirect(ci_l[:]))
         nc.vector.tensor_copy(xq_s[:], x_sc[:].indirect(offs_l[:]))
         for h in range(2):
             cols = offs_l[:, h * 16 : (h + 1) * 16]
@@ -204,20 +204,35 @@ def tile_picked_dwqiordd_none_p_kernel(
                 engine.tensor_tensor(res[:, cols], srt[t][:, cols], far[t][:, cols], ALU.subtract)
                 queue.dma_start(out_rows[:, t, cols], res[:, cols])
 
-        steps = [(0, 0, QUARTER), (0, QUARTER, HALF)] + [(t, 0, HALF) for t in range(1, PACK)]
+        def smaller(n, t, a, b):
+            lo = keep.tile([P, b - a], F32, name="lo%d" % n, tag="hid%d" % n, align_bytes=64)
+            nc.vector.tensor_tensor(lo[:], pa[t][:, a:b], pb[t][:, a:b], ALU.min)
+            return lo
+
+        def put(values, lst, t, a, b):
+            nc.vector.tensor_copy(srt[t][:].indirect(pairs(lst, a, b)), values)
+
+        steps = [(0, 0, QUARTER), (0, QUARTER, HALF), (1, 0, HALF), (2, 0, HALF), (3, 0, HALF)]
         for t in range(PACK):
             produce(t)
         larger(*steps[0])
-        for n, (t, a, b) in enumerate(steps):
-            nc.vector.tensor_copy(srt[t][:].indirect(pairs(n1_l, a, b)), hi[t][:, a:b])
-            lo = keep.tile([P, b - a], F32, name="lo%d" % n, tag="hid%d" % n, align_bytes=64)
-            nc.vector.tensor_tensor(lo[:], pa[t][:, a:b], pb[t][:, a:b], ALU.min)
-            for nxt in steps[n + 1 : n + 2]:
-                larger(*nxt)
-            nc.vector.tensor_copy(srt[t][:].indirect(pairs(n2_l, a, b)), lo[:])
+        for n, (t, a, b) in enumerate(steps[:3]):
+            put(hi[t][:, a:b], n1_l, t, a, b)
+            lo = smaller(n, t, a, b)
+            larger(*steps[n + 1])
+            put(lo[:], n2_l, t, a, b)
             if b == HALF:
                 look(t)
-            if t in (1, 2):
-                finish(nc.gpsimd, nc.gpsimd, t - 1, "pa%d" % t, 1)
+        finish(nc.gpsimd, nc.gpsimd, 0, "pa1", 1)
+        put(hi[2][:], n1_l, 2, 0, HALF)
+        larger(*steps[4])
+        lo2 = smaller(3, *steps[3])
+        lo3 = smaller(4, *steps[4])
+        put(hi[3][:], n1_l, 3, 0, HALF)
+        put(lo2[:], n2_l, 2, 0, HALF)
+        look(2)
+        finish(nc.gpsimd, nc.gpsimd, 1, "pa3", 1)
+        put(lo3[:], n2_l, 3, 0, HALF)
+        look(3)
         finish(nc.vector, nc.sync, 2, "hid4", 1)
         finish(nc.vector, nc.sync, 3, "res3", 2)

@@ -59,7 +59,7 @@ def tile_picked_dwqiordd_none_p_kernel(
         for j in range(2):
             nc.sync.dma_start(d_sc[:].bitcast(I32)[j:P:16, :], d_rows2[j])
         for j in range(2, 4):
-            nc.scalar.dma_start(d_sc[:].bitcast(I32)[j:P:32, :], d_rows4[j])
+            nc.sync.dma_start(d_sc[:].bitcast(I32)[j:P:32, :], d_rows4[j])
         nc.sync.dma_start(d_w[:].bitcast(I32), words_of(d_words))
         offs_l = load_list(offs, "offs_l")
         for j in range(4):

from contextlib import ExitStack

import concourse.mybir as mybir

F32 = mybir.dt.float32
BF16 = mybir.dt.bfloat16
I32 = mybir.dt.int32
U32 = mybir.dt.uint32
U16 = mybir.dt.uint16
U8 = mybir.dt.uint8
FP8X4 = mybir.dt.float8_e4m3fn_x4
ALU = mybir.AluOpType
COPY = mybir.ActivationFunctionType.Copy

P = 128
PACK = 4
TABLE = 2048
S = 512
HALF = 256
QUARTER = 128
SIXTEENTH = 0.0625
FLOPS = 2 * 2 * 512 * 512 * 512


def tile_picked_dwqiordd_none_p_kernel(
    tc, x_words, x_scales, d_words, d_scales, gs, offs, ci, k1, n1, n2, n3, out
):
    nc = tc.nc
    with ExitStack() as ctx:
        keep = ctx.enter_context(tc.tile_pool(name="keep", bufs=1))
        psum = ctx.enter_context(tc.psum_pool(name="psum", bufs=1))

        def load_list(src, name):
            tile = keep.tile([P, src.shape[1]], U16, name=name)
            nc.sync.dma_start(tile[:], src)
            return tile

        def words_of(src):
            return src[0].rearrange("p n t -> p (n t)").bitcast(I32)

        def dealt(ap):
            return ap.rearrange("p (t m) -> p m t", t=PACK)

        def in_order(ap):
            return ap.rearrange("p (m t) -> p m t", t=PACK)

        d_sc = keep.tile([P, TABLE], U8, name="d_sc")
        x_sc = keep.tile([P, TABLE], U8, name="x_sc")
        d_w = keep.tile([P, TABLE], U32, name="d_w")
        x_w = keep.tile([P, TABLE], U32, name="x_w", tag="x_w")
        nc.vector.memset(d_sc[:].bitcast(I32), 0)
        nc.vector.memset(x_sc[:].bitcast(I32), 0)

        ci_l = load_list(ci, "ci_l")
        k1_l = load_list(k1, "k1_l")
        d_rows2 = d_scales[0].bitcast(I32).rearrange("(m j) c -> j m c", j=2)
        d_rows4 = d_scales[0].bitcast(I32).rearrange("(q j) c -> j q c", j=4)
        x_rows4 = x_scales[0].bitcast(I32).rearrange("(q j) c -> j q c", j=4)
        for j in range(2):
            nc.sync.dma_start(d_sc[:].bitcast(I32)[j:P:16, :], d_rows2[j])
        for j in range(2, 4):
            nc.sync.dma_start(d_sc[:].bitcast(I32)[j:P:32, :], d_rows4[j])
        nc.sync.dma_start(d_w[:].bitcast(I32), words_of(d_words))
        offs_l = load_list(offs, "offs_l")
        for j in range(4):
            nc.sync.dma_start(x_sc[:].bitcast(I32)[j:P:32, :], x_rows4[j])
        nc.sync.dma_start(x_w[:].bitcast(I32), words_of(x_words))
        gs_t = keep.tile([P, PACK], F32, name="gs_t")
        nc.sync.dma_start(gs_t[:], gs.rearrange("(p t) o -> p (t o)", t=PACK))
        n1_l = load_list(n1, "n1_l")
        n2_l = load_list(n2, "n2_l")
        n3_l = load_list(n3, "n3_l")

        gain = keep.tile([P, PACK], F32, name="gain")
        nc.scalar.activation(gain[:], gs_t[:], COPY, scale=SIXTEENTH)

        ci_s = keep.tile([P, S], U8, name="ci_s", align_bytes=64)
        ci_w = keep.tile([P, S], U32, name="ci_w", align_bytes=64)
        k1_sg = keep.tile([P, S], U8, name="k1_sg")
        k1_w0 = keep.tile([P, P], U32, name="k1_w0", align_bytes=64)
        xq_s = keep.tile([P, S], U8, name="xq_s", align_bytes=64)
        xq_w = [keep.tile([P, HALF], U32, name="xq_w%d" % h, align_bytes=64) for h in range(2)]

        nc.vector.tensor_copy(k1_sg[:], d_sc[:].indirect(k1_l[:]))
        nc.vector.tensor_copy(dealt(ci_s[:]), d_sc[:].indirect(ci_l[:]))
        k1_s = keep.tile([P, S], U8, name="k1_s", align_bytes=64)
        nc.vector.tensor_copy(dealt(k1_s[:]), in_order(k1_sg[:]))
        for j in range(2):
            nc.sync.dma_start(k1_s[:].bitcast(I32)[2 + j : P : 32, :], k1_s[:].bitcast(I32)[16 + j : P : 32, :])
        nc.vector.tensor_copy(dealt(ci_w[:]), d_w[:].indirect(ci_l[:]))
        nc.vector.tensor_copy(xq_s[:], x_sc[:].indirect(offs_l[:]))
        for h in range(2):
            cols = offs_l[:, h * 16 : (h + 1) * 16]
            nc.vector.tensor_copy(xq_w[h][:], x_w[:].indirect(cols))

        def score(dst, t, h, lo, n):
            nc.tensor.matmul_mx(
                out=dst,
                lhsT=ci_w[:, t * P : (t + 1) * P].bitcast(FP8X4),
                lhsT_scale=ci_s[:, t * P : (t + 1) * P],
                rhs=xq_w[h][:, lo : lo + n].bitcast(FP8X4),
                rhs_scale=xq_s[:, h * HALF + lo : h * HALF + lo + n],
                start=True,
                stop=True,
            )

        z_in = [keep.tile([P, HALF, PACK], BF16, name="z_in%d" % h, tag="hid%d" % (5 * h), align_bytes=64) for h in range(2)]
        z_rows = keep.tile([P, PACK, HALF], BF16, name="z_rows", tag="z_rows", align_bytes=64)
        for u in range(2):
            bank = psum.tile([P, 2, HALF], F32, name="s_a%d" % u)
            for v in range(2):
                score(bank[:, v, :], 2 * u + v, 0, 0, HALF)
            for v in range(2):
                t = 2 * u + v
                nc.scalar.activation(z_rows[:, t, :], bank[:, v, :], COPY, scale=gain[:, t : t + 1])
        nc.scalar.copy(z_in[0][:], z_rows[:].rearrange("p t j -> p j t"))

        k1_wg = keep.tile([P, S], U32, name="k1_wg", tag="x_w")
        nc.vector.tensor_copy(k1_wg[:], d_w[:].indirect(k1_l[:]))
        nc.vector.tensor_copy(k1_w0[:], in_order(k1_wg[:])[:, :, 0])

        for u in range(2):
            bank = psum.tile([P, PACK, QUARTER], F32, name="s_b%d" % u)
            for t in range(PACK):
                score(bank[:, t, :], t, 1, u * QUARTER, QUARTER)
            nc.vector.tensor_tensor(
                z_in[1][:, u * QUARTER : (u + 1) * QUARTER, :],
                bank[:].rearrange("p t j -> p j t"),
                gain[:].unsqueeze(1).to_broadcast([P, QUARTER, PACK]),
                ALU.mult,
            )

        z_w = keep.tile([P, S], U32, name="z_w", align_bytes=64)
        z_s = keep.tile([P, S], U8, name="z_s", align_bytes=64)
        for h, a, b in ((1, 0, QUARTER), (1, QUARTER, HALF), (0, 0, HALF)):
            nc.vector.quantize_mx(
                out=z_w[:, h * HALF + a : h * HALF + b].bitcast(FP8X4),
                scales=z_s[:, h * HALF + a : h * HALF + b],
                in_=z_in[h][:, a:b, :].rearrange("p j t -> p (j t)"),
            )
        k1_wr = keep.tile([P, PACK - 1, P], U32, name="k1_wr", tag="z_rows", align_bytes=64)
        nc.vector.tensor_copy(k1_wr[:].rearrange("p t m -> p m t"), in_order(k1_wg[:])[:, :, 1:])
        k1_w = [k1_w0[:]] + [k1_wr[:, t, :] for t in range(PACK - 1)]

        def layer(dst, t, lo, n):
            nc.tensor.matmul_mx(
                out=dst,
                lhsT=k1_w[t].bitcast(FP8X4),
                lhsT_scale=k1_s[:, t * P : (t + 1) * P],
                rhs=z_w[:, lo : lo + n].bitcast(FP8X4),
                rhs_scale=z_s[:, lo : lo + n],
                start=True,
                stop=True,
            )

        out_rows = out.rearrange("(p t) j -> p t j", t=PACK)
        hid = [keep.tile([P, S], F32, name="hid%d" % t, tag="hid%d" % t, align_bytes=64) for t in range(PACK)]
        pa = [keep.tile([P, HALF], F32, name="pa%d" % t, tag="pa%d" % t, align_bytes=64) for t in range(PACK)]
        pb = [keep.tile([P, HALF], F32, name="pb%d" % t) for t in range(PACK)]
        hi = [keep.tile([P, HALF], F32, name="hi%d" % t) for t in range(PACK)]
        srt = [keep.tile([P, S], F32, name="srt%d" % t) for t in range(PACK)]
        far = [keep.tile([P, S], F32, name="far%d" % t) for t in range(PACK)]

        def pairs(lst, a, b):
            return lst[:, a // 16 : b // 16]

        def fetch(t, a, b, first):
            if first:
                nc.vector.tensor_copy(pa[t][:, a:b], hid[t][:].indirect(pairs(n1_l, a, b)))
            else:
                nc.scalar.activation(pa[t][:, a:b], hid[t][:].indirect(pairs(n1_l, a, b)), COPY)
            nc.scalar.activation(pb[t][:, a:b], hid[t][:].indirect(pairs(n2_l, a, b)), COPY)

        def produce(t):
            if t == 0:
                for h in (1, 0):
                    bank = psum.tile([P, S], F32, name="h_bank", tag="h%d" % (1 - h))
                    layer(bank[:, :HALF], t, h * HALF, HALF)
                    cols = slice(h * HALF, (h + 1) * HALF)
                    if h == 1:
                        nc.vector.tensor_scalar(hid[t][:, cols], bank[:, :HALF], SIXTEENTH, None, ALU.mult)
                    else:
                        nc.scalar.activation(hid[t][:, cols], bank[:, :HALF], COPY, scale=SIXTEENTH)
                fetch(t, 0, QUARTER, True)
                fetch(t, QUARTER, HALF, False)
            else:
                bank = psum.tile([P, S], F32, name="h_bank", tag="h1")
                layer(bank[:], t, 0, S)
                nc.scalar.activation(hid[t][:], bank[:], COPY, scale=SIXTEENTH)
                fetch(t, 0, HALF, False)

        def larger(t, a, b):
            nc.vector.tensor_tensor(hi[t][:, a:b], pa[t][:, a:b], pb[t][:, a:b], ALU.max)

        def look(t):
            for a in (0, HALF):
                nc.scalar.activation(far[t][:, a : a + HALF], srt[t][:].indirect(pairs(n3_l, a, a + HALF)), COPY)

        def finish(engine, queue, t, tag, pieces):
            res = keep.tile([P, S], F32, name="res%d" % t, tag=tag, align_bytes=64)
            width = S // pieces
            for a in range(0, S, width):
                cols = slice(a, a + width)
                engine.tensor_tensor(res[:, cols], srt[t][:, cols], far[t][:, cols], ALU.subtract)
                queue.dma_start(out_rows[:, t, cols], res[:, cols])

        def smaller(n, t, a, b):
            lo = keep.tile([P, b - a], F32, name="lo%d" % n, tag="hid%d" % n, align_bytes=64)
            nc.vector.tensor_tensor(lo[:], pa[t][:, a:b], pb[t][:, a:b], ALU.min)
            return lo

        def put(values, lst, t, a, b):
            nc.vector.tensor_copy(srt[t][:].indirect(pairs(lst, a, b)), values)

        steps = [(0, 0, QUARTER), (0, QUARTER, HALF), (1, 0, HALF), (2, 0, HALF), (3, 0, HALF)]
        for t in range(PACK):
            produce(t)
        larger(*steps[0])
        for n, (t, a, b) in enumerate(steps[:3]):
            put(hi[t][:, a:b], n1_l, t, a, b)
            lo = smaller(n, t, a, b)
            larger(*steps[n + 1])
            put(lo[:], n2_l, t, a, b)
            if b == HALF:
                look(t)
        finish(nc.gpsimd, nc.gpsimd, 0, "pa1", 1)
        put(hi[2][:], n1_l, 2, 0, HALF)
        larger(*steps[4])
        lo2 = smaller(3, *steps[3])
        lo3 = smaller(4, *steps[4])
        put(hi[3][:], n1_l, 3, 0, HALF)
        put(lo2[:], n2_l, 2, 0, HALF)
        look(2)
        finish(nc.gpsimd, nc.gpsimd, 1, "pa3", 1)
        put(lo3[:], n2_l, 3, 0, HALF)
        look(3)
        finish(nc.vector, nc.sync, 2, "hid4", 1)
        finish(nc.vector, nc.sync, 3, "res3", 2)
